import numpy as np
import ml_dtypes


def mxq(x, axis, fmt="e4m3"):
    dtype, down = {"e4m3": (ml_dtypes.float8_e4m3fn, 7), "e5m2": (ml_dtypes.float8_e5m2, 14)}[fmt]
    v = np.moveaxis(np.asarray(x, np.float32).astype(ml_dtypes.bfloat16).astype(np.float64), axis, -1)
    blocks = v.reshape(v.shape[:-1] + (-1, 32))
    amax = np.abs(blocks).max(-1, keepdims=True)
    byte = np.maximum(np.where(amax > 0, np.frexp(amax)[1] - 1 + 127, 0) - down, 1)
    scale = np.exp2(byte - 127.0)
    codes = (blocks / scale).astype(np.float32).astype(dtype).astype(np.float64)
    return np.moveaxis((codes * scale).reshape(v.shape), -1, axis)


WIDE = False


def mx_kscale(k):
    if not WIDE:
        return np.ones(k)
    levels = np.array([10, -10, 5, -5, 0])
    if k % 512:
        return np.exp2(np.random.permutation(np.resize(levels, k // 32))).repeat(32)
    a = np.empty((k // 512, 16))
    for p in range(k // 512):
        a[p, :8] = np.random.permutation(np.resize(levels, 8))
        for g in range(8):
            far = levels[np.abs(levels - a[p, g]) >= 10]
            a[p, g + 8] = far[np.random.randint(len(far))]
    return np.exp2(a.ravel()).repeat(32)


def f64(x):
    return np.asarray(x).astype(np.float64)


def striped(idx):
    return np.tile(idx.reshape(-1, 16).T, (8, 1)).astype(np.uint16)


def unstriped(offs):
    return offs[:16].T.reshape(-1).astype(np.int64)


def striped8(idx):
    return np.concatenate([x.reshape(-1, 16).T for x in idx]).astype(np.uint16)


def runs(offs, k):
    lists = np.stack([offs[16 * r : 16 * r + 16].T.reshape(-1) for r in range(8)]).astype(np.int64)
    return lists[np.arange(k) % 512 // 64]


def pack_weight(w):
    k, n = w.shape
    w = f64(np.asarray(w, np.float32).astype(ml_dtypes.bfloat16)).reshape(k // 32, 32, n)
    amax = np.abs(w).max(1)
    byte = np.clip(np.where(amax > 0, np.frexp(amax)[1] - 1 + 127 - 7, 1), 1, 254)
    scaled = (w * np.exp2(127.0 - byte)[:, None, :]).reshape(k, n).astype(np.float32)
    words = np.ascontiguousarray(scaled.reshape(k // 512, 128, 4, n).transpose(0, 1, 3, 2)).astype(ml_dtypes.float8_e4m3fn).view(np.uint8)
    return words, np.ascontiguousarray(byte.astype(np.uint8).reshape(k // 512, 16, n))


def unpack_weight(words, scales):
    g, p, n, _ = words.shape
    vals = np.ascontiguousarray(words).view(ml_dtypes.float8_e4m3fn).astype(np.float64) * np.repeat(np.exp2(scales.astype(np.float64) - 127.0), 8, axis=1)[..., None]
    return vals.transpose(0, 1, 3, 2).reshape(g * 512, n)


def sigmoid(v):
    return 1.0 / (1.0 + np.exp(-np.maximum(v, -700.0)))


K, T, S, N, H = 512, 2048, 512, 512, 512


def setup_inputs():
    n = np.random.standard_normal
    s = mx_kscale(K)[:, None]
    u = mx_kscale(H)
    packed_xT = pack_weight(n((K, T)) * s)
    return {
        "x_words": packed_xT[0],
        "x_scales": packed_xT[1],
        "w1": (n((K, H)) / np.sqrt(K) / s).astype(np.float32),
        "w2": (n((K, H)) / np.sqrt(K) / s).astype(np.float32),
        "gn": (np.random.uniform(0.5, 1.5, (H, 1)) * u[:, None]).astype(np.float32),
        "w3": (n((H, N)) / np.sqrt(H) / u[:, None]).astype(np.float32),
        "offs": striped(np.random.permutation(T)[:S]),
        "two": striped(np.random.permutation(T)[:S]),
        "n1": striped8(np.stack([np.random.permutation(S) for _ in range(8)])),
        "n2": striped8(np.stack([np.random.permutation(S) for _ in range(8)])),
        "n3": striped8(np.stack([np.random.permutation(S) for _ in range(8)])),
        "n4": striped8(np.stack([np.random.permutation(S) for _ in range(8)])),
        "n5": striped8(np.stack([np.random.permutation(S) for _ in range(8)])),
    }


def reference(x_words, x_scales, w1, w2, gn, w3, offs, two, n1, n2, n3, n4, n5):
    xq = unpack_weight(x_words, x_scales)[:, unstriped(offs)]
    y = mxq(f64(w1), 0, "e4m3").T @ xq
    x_two = unpack_weight(x_words, x_scales)[:, unstriped(two)]
    d = mxq(f64(w2), 0, "e4m3").T @ x_two
    z = f64(gn) * (y + (sigmoid(d[np.arange(H)[:, None], runs(n2, H)] - d)) * (y[np.arange(H)[:, None], runs(n1, H)] - y))
    h = mxq(f64(w3), 0, "e4m3").T @ mxq(z, 0, "e4m3")
    pa = h[np.arange(N)[:, None], runs(n3, N)]
    return pa + (sigmoid(h[np.arange(N)[:, None], runs(n4, N)])) * (h[np.arange(N)[:, None], runs(n5, N)] - pa)

@@ -1,0 +1,148 @@
+from contextlib import ExitStack
+
+import concourse.mybir as mybir
+
+K, T, S, H, N = 512, 2048, 512, 512, 512
+FLOPS = 2 * K * H * S * 2 + 2 * H * N * S
+
+F32 = mybir.dt.float32
+BF16 = mybir.dt.bfloat16
+I32 = mybir.dt.int32
+U32 = mybir.dt.uint32
+U16 = mybir.dt.uint16
+U8 = mybir.dt.uint8
+FP8X4 = mybir.dt.float8_e4m3fn_x4
+ACT = mybir.ActivationFunctionType
+ALU = mybir.AluOpType
+
+P = 128
+PACK = 4
+HALF = S // 2
+
+
+def tile_picked_twlpullblerp_none_p_kernel(tc, x_words, x_scales, w1, w2, gn, w3, offs, two, n1, n2, n3, n4, n5, out):
+    nc = tc.nc
+    with ExitStack() as ctx:
+        keep = ctx.enter_context(tc.tile_pool(name="keep", bufs=1))
+        psum = ctx.enter_context(tc.psum_pool(name="psum", bufs=8))
+
+        def load_list(src, name):
+            tile = keep.tile([P, S // 16], U16, name=name)
+            nc.sync.dma_start(tile[:], src)
+            return tile
+
+        def load_weight(w, name):
+            raw = keep.tile([P, PACK, 512], F32, name=name)
+            nc.sync.dma_start(out=raw[:], in_=w.rearrange("(p j) c -> p j c", j=PACK))
+            return raw
+
+        def deal(raw, name, copy):
+            dealt = keep.tile([P, PACK * 512], BF16, name=name, align_bytes=64)
+            copy(out=dealt[:].rearrange("p (t m j) -> p m t j", t=PACK, j=PACK), in_=raw[:].rearrange("p j (m t) -> p m t j", t=PACK))
+            return dealt
+
+        def quantize(values, name):
+            width = values.shape[1] // PACK
+            codes = keep.tile([P, width], U32, name=name + "_codes", align_bytes=64)
+            scales = keep.tile([P, width], U8, name=name + "_scales", align_bytes=64)
+            nc.vector.quantize_mx(out=codes[:].bitcast(FP8X4), scales=scales[:], in_=values)
+            return codes, scales
+
+        def product(weight, t, moving, name):
+            width = moving[0].shape[1]
+            bank = psum.tile([P, width], F32, name=name, tag="bank")
+            cols = slice(t * P, (t + 1) * P)
+            nc.tensor.matmul_mx(out=bank[:], lhsT=weight[0][:, cols].bitcast(FP8X4), lhsT_scale=weight[1][:, cols],
+                                rhs=moving[0][:].bitcast(FP8X4), rhs_scale=moving[1][:], start=True, stop=True)
+            return bank
+
+        def pick(window, offsets, dtype, name):
+            picked = keep.tile([P, S], dtype, name=name, align_bytes=64)
+            nc.vector.tensor_copy(picked[:], window[:].indirect(offsets[:]))
+            return picked
+
+        x_bytes = keep.tile([P, T], U8, name="x_bytes")
+        nc.vector.memset(x_bytes[:].bitcast(I32), 0)
+        warm = keep.tile([P, 1], F32, name="warm")
+        nc.vector.memset(warm[:], 0.0)
+        for q in range(4):
+            nc.scalar.dma_start(out=x_bytes[32 * q : 32 * q + 4, :].bitcast(I32), in_=x_scales[0, 4 * q : 4 * q + 4, :].bitcast(I32))
+        warmed = keep.tile([P, 1], F32, name="warmed")
+        nc.scalar.activation(warmed[:], warm[:], ACT.Sigmoid)
+        two_sb = load_list(two, "two_sb")
+        offs_sb = load_list(offs, "offs_sb")
+        w2_raw = load_weight(w2, "w2_raw")
+        x_codes = keep.tile([P, T], U32, name="x_codes")
+        nc.sync.dma_start(out=x_codes[:].bitcast(I32), in_=x_words[0].rearrange("p c r -> p (c r)").bitcast(I32))
+        n2_sb = load_list(n2, "n2_sb")
+        gain = keep.tile([P, PACK], F32, name="gain")
+        nc.sync.dma_start(out=gain[:], in_=gn.rearrange("(p t) o -> p (t o)", t=PACK))
+        n1_sb = load_list(n1, "n1_sb")
+        w1_raw = load_weight(w1, "w1_raw")
+        w3_raw = load_weight(w3, "w3_raw")
+        n4_sb = load_list(n4, "n4_sb")
+        n5_sb = load_list(n5, "n5_sb")
+        n3_sb = load_list(n3, "n3_sb")
+
+        two_bytes = pick(x_bytes, two_sb, U8, "two_bytes")
+        idx_bytes = pick(x_bytes, offs_sb, U8, "idx_bytes")
+        w2_dealt = deal(w2_raw, "w2_dealt", nc.scalar.copy)
+        w2_q = quantize(w2_dealt[:], "w2")
+        two_codes = pick(x_codes, two_sb, U32, "two_codes")
+        idx_codes = pick(x_codes, offs_sb, U32, "idx_codes")
+        d_banks = [product(w2_q, t, (two_codes, two_bytes), f"d_bank{t}") for t in range(PACK)]
+        w1_dealt = deal(w1_raw, "w1_dealt", nc.vector.tensor_copy)
+        w1_q = quantize(w1_dealt[:], "w1")
+        y_banks = [product(w1_q, t, (idx_codes, idx_bytes), f"y_bank{t}") for t in range(PACK)]
+
+        pulled = keep.tile([P, PACK, S], F32, name="pulled")
+        stayed = keep.tile([P, PACK, S], F32, name="stayed")
+        for t in range(PACK):
+            d_win = keep.tile([P, 2 * S], F32, name=f"d_win{t}")
+            d_own = keep.tile([P, S], F32, name=f"d_own{t}")
+            nc.scalar.copy(d_win[:, :S], d_banks[t][:])
+            nc.scalar.copy(d_own[:], d_banks[t][:])
+            gap = keep.tile([P, S], F32, name=f"gap{t}")
+            nc.vector.tensor_tensor(gap[:], d_win[:].indirect(n2_sb[:]), d_own[:], ALU.subtract)
+            gate = keep.tile([P, S], F32, name=f"gate{t}")
+            nc.scalar.activation(gate[:], gap[:], ACT.Sigmoid)
+            y_win = keep.tile([P, 2 * S], F32, name=f"y_win{t}")
+            nc.scalar.activation(y_win[:, :S], y_banks[t][:], ACT.Copy, scale=gain[:, t : t + 1])
+            nc.vector.tensor_tensor(pulled[:, t, :], y_win[:].indirect(n1_sb[:]), gate[:], ALU.mult)
+            nc.vector.scalar_tensor_tensor(stayed[:, t, :], gate[:], 1.0, y_win[:, :S], ALU.subtract, ALU.mult)
+
+        w3_dealt = deal(w3_raw, "w3_dealt", nc.scalar.copy)
+        w3_q = quantize(w3_dealt[:], "w3")
+
+        h_wins = [keep.tile([P, 2 * S], F32, name=f"h_win{t}") for t in range(PACK)]
+        zs = []
+        for c in range(2):
+            cols = slice(c * HALF, (c + 1) * HALF)
+            z = keep.tile([P, HALF * PACK], BF16, name=f"z{c}", align_bytes=64)
+            nc.vector.tensor_tensor(
+                z[:].rearrange("p (c i t) -> p c t i", i=4, t=PACK),
+                pulled[:, :, cols].rearrange("p t (c i) -> p c t i", i=4),
+                stayed[:, :, cols].rearrange("p t (c i) -> p c t i", i=4),
+                ALU.subtract,
+            )
+            zs.append(z)
+        for c in range(2):
+            cols = slice(c * HALF, (c + 1) * HALF)
+            z_q = quantize(zs[c][:], f"z{c}")
+            for t in range(PACK):
+                bank = product(w3_q, t, z_q, f"h_bank{c}{t}")
+                nc.scalar.copy(h_wins[t][:, cols], bank[:])
+
+        out_rows = out.rearrange("(p t) j -> t p j", t=PACK)
+        for t in range(PACK):
+            mix = keep.tile([P, S], F32, name=f"mix{t}")
+            nc.scalar.activation(mix[:], h_wins[t][:].indirect(n4_sb[:]), ACT.Sigmoid)
+            rest = keep.tile([P, S], F32, name=f"rest{t}")
+            nc.scalar.activation(rest[:], mix[:], ACT.Copy, bias=1.0, scale=-1.0)
+            far = keep.tile([P, S], F32, name=f"far{t}")
+            nc.vector.tensor_tensor(far[:], h_wins[t][:].indirect(n5_sb[:]), mix[:], ALU.mult)
+            near = keep.tile([P, S], F32, name=f"near{t}")
+            nc.vector.tensor_tensor(near[:], h_wins[t][:].indirect(n3_sb[:]), rest[:], ALU.mult)
+            res = keep.tile([P, S], F32, name=f"res{t}")
+            nc.vector.tensor_tensor(res[:], far[:], near[:], ALU.add)
+            nc.sync.dma_start(out=out_rows[t], in_=res[:])

@@ -26,20 +26,23 @@ def tile_picked_twlpullblerp_none_p_kernel(tc, x_words, x_scales, w1, w2, gn, w3
         keep = ctx.enter_context(tc.tile_pool(name="keep", bufs=1))
         psum = ctx.enter_context(tc.psum_pool(name="psum", bufs=8))
 
+        def clock(ap, name):
+            tick = keep.tile([P, 1], ap.dtype, name=name)
+            nc.gpsimd.tensor_copy(tick[:], ap)
+
         def load_list(src, name):
             tile = keep.tile([P, S // 16], U16, name=name)
             nc.sync.dma_start(tile[:], src)
             return tile
 
-        def load_weight(w, name):
-            raw = keep.tile([P, PACK, 512], F32, name=name)
-            nc.sync.dma_start(out=raw[:], in_=w.rearrange("(p j) c -> p j c", j=PACK))
+        def load_columns(w, first, width, name):
+            raw = keep.tile([P, PACK, width], F32, name=name)
+            nc.sync.dma_start(out=raw[:], in_=w[:, first : first + width].rearrange("(p j) c -> p j c", j=PACK))
             return raw
 
-        def deal(raw, name, copy):
-            dealt = keep.tile([P, PACK * 512], BF16, name=name, align_bytes=64)
-            copy(out=dealt[:].rearrange("p (t m j) -> p m t j", t=PACK, j=PACK), in_=raw[:].rearrange("p j (m t) -> p m t j", t=PACK))
-            return dealt
+        def deal(dealt, first, raw, copy):
+            ms = slice(first // PACK, (first + raw.shape[2]) // PACK)
+            copy(out=dealt[:].rearrange("p (t m j) -> p m t j", t=PACK, j=PACK)[:, ms], in_=raw.rearrange("p j (m t) -> p m t j", t=PACK))
 
         def quantize(values, name):
             width = values.shape[1] // PACK
@@ -56,8 +59,8 @@ def tile_picked_twlpullblerp_none_p_kernel(tc, x_words, x_scales, w1, w2, gn, w3
                                 rhs=moving[0][:].bitcast(FP8X4), rhs_scale=moving[1][:], start=True, stop=True)
             return bank
 
-        def pick(window, offsets, dtype, name):
-            picked = keep.tile([P, S], dtype, name=name, align_bytes=64)
+        def pick(window, offsets, dtype, name, tag=None):
+            picked = keep.tile([P, S], dtype, name=name, tag=tag or name, align_bytes=64)
             nc.vector.tensor_copy(picked[:], window[:].indirect(offsets[:]))
             return picked
 
@@ -70,51 +73,67 @@ def tile_picked_twlpullblerp_none_p_kernel(tc, x_words, x_scales, w1, w2, gn, w3
         warmed = keep.tile([P, 1], F32, name="warmed")
         nc.scalar.activation(warmed[:], warm[:], ACT.Sigmoid)
         two_sb = load_list(two, "two_sb")
-        offs_sb = load_list(offs, "offs_sb")
-        w2_raw = load_weight(w2, "w2_raw")
         x_codes = keep.tile([P, T], U32, name="x_codes")
         nc.sync.dma_start(out=x_codes[:].bitcast(I32), in_=x_words[0].rearrange("p c r -> p (c r)").bitcast(I32))
+        offs_sb = load_list(offs, "offs_sb")
+        w2_raw = [load_columns(w2, c * HALF, HALF, f"w2_raw{c}") for c in range(2)]
+        w1_raw = [load_columns(w1, c * HALF, HALF, f"w1_raw{c}") for c in range(2)]
         n2_sb = load_list(n2, "n2_sb")
         gain = keep.tile([P, PACK], F32, name="gain")
         nc.sync.dma_start(out=gain[:], in_=gn.rearrange("(p t) o -> p (t o)", t=PACK))
         n1_sb = load_list(n1, "n1_sb")
-        w1_raw = load_weight(w1, "w1_raw")
-        w3_raw = load_weight(w3, "w3_raw")
+        w3_raw = load_columns(w3, 0, N, "w3_raw")
         n4_sb = load_list(n4, "n4_sb")
         n5_sb = load_list(n5, "n5_sb")
         n3_sb = load_list(n3, "n3_sb")
 
-        two_bytes = pick(x_bytes, two_sb, U8, "two_bytes")
-        idx_bytes = pick(x_bytes, offs_sb, U8, "idx_bytes")
-        w2_dealt = deal(w2_raw, "w2_dealt", nc.scalar.copy)
-        w2_q = quantize(w2_dealt[:], "w2")
         two_codes = pick(x_codes, two_sb, U32, "two_codes")
+        two_bytes = pick(x_bytes, two_sb, U8, "two_bytes")
         idx_codes = pick(x_codes, offs_sb, U32, "idx_codes")
+        w2_dealt = keep.tile([P, PACK * H], BF16, name="w2_dealt", align_bytes=64)
+        for c in range(2):
+            deal(w2_dealt, c * HALF, w2_raw[c][:], nc.scalar.copy)
+        w2_q = quantize(w2_dealt[:], "w2")
+        idx_bytes = pick(x_bytes, offs_sb, U8, "idx_bytes", tag="w2_dealt")
         d_banks = [product(w2_q, t, (two_codes, two_bytes), f"d_bank{t}") for t in range(PACK)]
-        w1_dealt = deal(w1_raw, "w1_dealt", nc.vector.tensor_copy)
+        w1_dealt = keep.tile([P, PACK * H], BF16, name="w1_dealt", align_bytes=64)
+        deal(w1_dealt, 0, w1_raw[0][:], nc.scalar.copy)
+        deal(w1_dealt, HALF, w1_raw[1][:], nc.vector.tensor_copy)
         w1_q = quantize(w1_dealt[:], "w1")
         y_banks = [product(w1_q, t, (idx_codes, idx_bytes), f"y_bank{t}") for t in range(PACK)]
 
         pulled = keep.tile([P, PACK, S], F32, name="pulled")
         stayed = keep.tile([P, PACK, S], F32, name="stayed")
-        for t in range(PACK):
+        w3_dealt = keep.tile([P, PACK * N], BF16, name="w3_dealt", align_bytes=64)
+        gaps = []
+
+        def gap_of_d(t):
             d_win = keep.tile([P, 2 * S], F32, name=f"d_win{t}")
             d_own = keep.tile([P, S], F32, name=f"d_own{t}")
             nc.scalar.copy(d_win[:, :S], d_banks[t][:])
             nc.scalar.copy(d_own[:], d_banks[t][:])
             gap = keep.tile([P, S], F32, name=f"gap{t}")
             nc.vector.tensor_tensor(gap[:], d_win[:].indirect(n2_sb[:]), d_own[:], ALU.subtract)
-            gate = keep.tile([P, S], F32, name=f"gate{t}")
-            nc.scalar.activation(gate[:], gap[:], ACT.Sigmoid)
+            gaps.append(gap)
+
+        def blend_y(t):
             y_win = keep.tile([P, 2 * S], F32, name=f"y_win{t}")
             nc.scalar.activation(y_win[:, :S], y_banks[t][:], ACT.Copy, scale=gain[:, t : t + 1])
+            gate = keep.tile([P, S], F32, name=f"gate{t}")
+            nc.scalar.activation(gate[:], gaps[t][:], ACT.Sigmoid)
             nc.vector.tensor_tensor(pulled[:, t, :], y_win[:].indirect(n1_sb[:]), gate[:], ALU.mult)
             nc.vector.scalar_tensor_tensor(stayed[:, t, :], gate[:], 1.0, y_win[:, :S], ALU.subtract, ALU.mult)
 
-        w3_dealt = deal(w3_raw, "w3_dealt", nc.scalar.copy)
+        gap_of_d(0)
+
+        gap_of_d(1)
+        for t in range(PACK):
+            blend_y(t)
+            if t + 2 < PACK:
+                gap_of_d(t + 2)
+            deal(w3_dealt, t * P, w3_raw[:, :, t * P : (t + 1) * P], nc.scalar.copy)
         w3_q = quantize(w3_dealt[:], "w3")
 
-        h_wins = [keep.tile([P, 2 * S], F32, name=f"h_win{t}") for t in range(PACK)]
         zs = []
         for c in range(2):
             cols = slice(c * HALF, (c + 1) * HALF)
@@ -126,23 +145,38 @@ def tile_picked_twlpullblerp_none_p_kernel(tc, x_words, x_scales, w1, w2, gn, w3
                 ALU.subtract,
             )
             zs.append(z)
-        for c in range(2):
-            cols = slice(c * HALF, (c + 1) * HALF)
-            z_q = quantize(zs[c][:], f"z{c}")
-            for t in range(PACK):
-                bank = product(w3_q, t, z_q, f"h_bank{c}{t}")
-                nc.scalar.copy(h_wins[t][:, cols], bank[:])
+        z_q = [quantize(zs[c][:], f"z{c}") for c in range(2)]
 
         out_rows = out.rearrange("(p t) j -> t p j", t=PACK)
         for t in range(PACK):
+            h_win = keep.tile([P, 2 * S], F32, name=f"h_win{t}")
+            for c in range(2):
+                bank = product(w3_q, t, z_q[c], f"h_bank{c}{t}")
+                nc.scalar.copy(h_win[:, c * HALF : (c + 1) * HALF], bank[:])
+
             mix = keep.tile([P, S], F32, name=f"mix{t}")
-            nc.scalar.activation(mix[:], h_wins[t][:].indirect(n4_sb[:]), ACT.Sigmoid)
-            rest = keep.tile([P, S], F32, name=f"rest{t}")
-            nc.scalar.activation(rest[:], mix[:], ACT.Copy, bias=1.0, scale=-1.0)
             far = keep.tile([P, S], F32, name=f"far{t}")
-            nc.vector.tensor_tensor(far[:], h_wins[t][:].indirect(n5_sb[:]), mix[:], ALU.mult)
             near = keep.tile([P, S], F32, name=f"near{t}")
-            nc.vector.tensor_tensor(near[:], h_wins[t][:].indirect(n3_sb[:]), rest[:], ALU.mult)
             res = keep.tile([P, S], F32, name=f"res{t}")
-            nc.vector.tensor_tensor(res[:], far[:], near[:], ALU.add)
-            nc.sync.dma_start(out=out_rows[t], in_=res[:])
+            if t == 0:
+                pa = keep.tile([P, S], F32, name="pa")
+                nc.vector.tensor_copy(pa[:], h_win[:].indirect(n3_sb[:]))
+                nc.scalar.activation(mix[:], h_win[:].indirect(n4_sb[:]), ACT.Sigmoid)
+                nc.vector.tensor_tensor(far[:], h_win[:].indirect(n5_sb[:]), mix[:], ALU.mult)
+                nc.vector.scalar_tensor_tensor(near[:], mix[:], 1.0, pa[:], ALU.subtract, ALU.mult)
+                nc.vector.tensor_tensor(res[:], far[:], near[:], ALU.subtract)
+            else:
+                nc.scalar.activation(mix[:], h_win[:].indirect(n4_sb[:]), ACT.Sigmoid)
+                rest = keep.tile([P, S], F32, name=f"rest{t}")
+                nc.scalar.activation(rest[:], mix[:], ACT.Copy, bias=1.0, scale=-1.0)
+                nc.vector.tensor_tensor(far[:], h_win[:].indirect(n5_sb[:]), mix[:], ALU.mult)
+                nc.vector.tensor_tensor(near[:], h_win[:].indirect(n3_sb[:]), rest[:], ALU.mult)
+                if t < PACK - 1:
+                    nc.vector.tensor_tensor(res[:], far[:], near[:], ALU.add)
+            if t < PACK - 1:
+                nc.sync.dma_start(out=out_rows[t], in_=res[:])
+            else:
+                for c in range(2):
+                    cols = slice(c * HALF, (c + 1) * HALF)
+                    nc.vector.tensor_tensor(res[:, cols], far[:, cols], near[:, cols], ALU.add)
+                    nc.sync.dma_start(out=out_rows[t][:, cols], in_=res[:, cols])

@@ -1,6 +1,7 @@
 from contextlib import ExitStack
 
 import concourse.mybir as mybir
+from concourse.masks import make_identity
 
 K, T, S, H, N = 512, 2048, 512, 512, 512
 FLOPS = 2 * K * H * S * 2 + 2 * H * N * S
@@ -25,10 +26,6 @@ def tile_picked_twlpullblerp_none_p_kernel(tc, x_words, x_scales, w1, w2, gn, w3
     with ExitStack() as ctx:
         keep = ctx.enter_context(tc.tile_pool(name="keep", bufs=1))
         psum = ctx.enter_context(tc.psum_pool(name="psum", bufs=8))
-
-        def clock(ap, name):
-            tick = keep.tile([P, 1], ap.dtype, name=name)
-            nc.gpsimd.tensor_copy(tick[:], ap)
 
         def load_list(src, name):
             tile = keep.tile([P, S // 16], U16, name=name)
@@ -72,6 +69,8 @@ def tile_picked_twlpullblerp_none_p_kernel(tc, x_words, x_scales, w1, w2, gn, w3
             nc.scalar.dma_start(out=x_bytes[32 * q : 32 * q + 4, :].bitcast(I32), in_=x_scales[0, 4 * q : 4 * q + 4, :].bitcast(I32))
         warmed = keep.tile([P, 1], F32, name="warmed")
         nc.scalar.activation(warmed[:], warm[:], ACT.Sigmoid)
+        identity = keep.tile([P, P], F32, name="identity")
+        make_identity(nc, identity[:])
         two_sb = load_list(two, "two_sb")
         x_codes = keep.tile([P, T], U32, name="x_codes")
         nc.sync.dma_start(out=x_codes[:].bitcast(I32), in_=x_words[0].rearrange("p c r -> p (c r)").bitcast(I32))
@@ -148,35 +147,53 @@ def tile_picked_twlpullblerp_none_p_kernel(tc, x_words, x_scales, w1, w2, gn, w3
         z_q = [quantize(zs[c][:], f"z{c}") for c in range(2)]
 
         out_rows = out.rearrange("(p t) j -> t p j", t=PACK)
+        fars, nears = [], []
         for t in range(PACK):
             h_win = keep.tile([P, 2 * S], F32, name=f"h_win{t}")
             for c in range(2):
                 bank = product(w3_q, t, z_q[c], f"h_bank{c}{t}")
                 nc.scalar.copy(h_win[:, c * HALF : (c + 1) * HALF], bank[:])
-
             mix = keep.tile([P, S], F32, name=f"mix{t}")
             far = keep.tile([P, S], F32, name=f"far{t}")
             near = keep.tile([P, S], F32, name=f"near{t}")
-            res = keep.tile([P, S], F32, name=f"res{t}")
             if t == 0:
                 pa = keep.tile([P, S], F32, name="pa")
-                nc.vector.tensor_copy(pa[:], h_win[:].indirect(n3_sb[:]))
-                nc.scalar.activation(mix[:], h_win[:].indirect(n4_sb[:]), ACT.Sigmoid)
-                nc.vector.tensor_tensor(far[:], h_win[:].indirect(n5_sb[:]), mix[:], ALU.mult)
+                nc.vector.tensor_scalar(pa[:], h_win[:].indirect(n3_sb[:]), -1.0, 0.0, ALU.mult, ALU.add)
+            nc.scalar.activation(mix[:], h_win[:].indirect(n4_sb[:]), ACT.Sigmoid)
+            nc.vector.tensor_tensor(far[:], h_win[:].indirect(n5_sb[:]), mix[:], ALU.mult)
+            if t == 0:
                 nc.vector.scalar_tensor_tensor(near[:], mix[:], 1.0, pa[:], ALU.subtract, ALU.mult)
-                nc.vector.tensor_tensor(res[:], far[:], near[:], ALU.subtract)
             else:
-                nc.scalar.activation(mix[:], h_win[:].indirect(n4_sb[:]), ACT.Sigmoid)
                 rest = keep.tile([P, S], F32, name=f"rest{t}")
                 nc.scalar.activation(rest[:], mix[:], ACT.Copy, bias=1.0, scale=-1.0)
-                nc.vector.tensor_tensor(far[:], h_win[:].indirect(n5_sb[:]), mix[:], ALU.mult)
                 nc.vector.tensor_tensor(near[:], h_win[:].indirect(n3_sb[:]), rest[:], ALU.mult)
-                if t < PACK - 1:
-                    nc.vector.tensor_tensor(res[:], far[:], near[:], ALU.add)
-            if t < PACK - 1:
+            fars.append(far)
+            nears.append(near)
+            if t == 2:
+                res = keep.tile([P, S], F32, name="res2")
+                nc.vector.tensor_tensor(res[:], far[:], near[:], ALU.add)
                 nc.sync.dma_start(out=out_rows[t], in_=res[:])
-            else:
+            if t == 3:
+                res = keep.tile([P, S], F32, name="res3")
                 for c in range(2):
                     cols = slice(c * HALF, (c + 1) * HALF)
                     nc.vector.tensor_tensor(res[:, cols], far[:, cols], near[:, cols], ALU.add)
                     nc.sync.dma_start(out=out_rows[t][:, cols], in_=res[:, cols])
+
+        blocks = [slice(b * P, (b + 1) * P) for b in range(S // P)]
+        turned = []
+        for t in range(2):
+            bank = psum.tile([P, S], F32, name=f"sum_bank{t}", tag="bank")
+            for block in blocks:
+                nc.tensor.matmul(bank[:, block], fars[t][:, block], identity[:], start=True, stop=False, is_transpose=True)
+                nc.tensor.matmul(bank[:, block], nears[t][:, block], identity[:], start=False, stop=True, is_transpose=True)
+            sums = keep.tile([P, S], F32, name=f"sums{t}")
+            nc.scalar.copy(sums[:], bank[:])
+            turned.append(sums)
+        for t in range(2):
+            bank = psum.tile([P, S], F32, name=f"back_bank{t}", tag="bank")
+            for block in blocks:
+                nc.tensor.transpose(bank[:, block], turned[t][:, block], identity[:])
+            res = keep.tile([P, S], F32, name=f"res{t}")
+            nc.scalar.copy(res[:], bank[:])
+            nc.scalar.dma_start(out=out_rows[t], in_=res[:])

from contextlib import ExitStack

import concourse.mybir as mybir
from concourse.masks import make_identity

K, T, S, H, N = 512, 2048, 512, 512, 512
FLOPS = 2 * K * H * S * 2 + 2 * H * N * S

F32 = mybir.dt.float32
BF16 = mybir.dt.bfloat16
I32 = mybir.dt.int32
U32 = mybir.dt.uint32
U16 = mybir.dt.uint16
U8 = mybir.dt.uint8
FP8X4 = mybir.dt.float8_e4m3fn_x4
ACT = mybir.ActivationFunctionType
ALU = mybir.AluOpType

P = 128
PACK = 4
HALF = S // 2


def tile_picked_twlpullblerp_none_p_kernel(tc, x_words, x_scales, w1, w2, gn, w3, offs, two, n1, n2, n3, n4, n5, out):
    nc = tc.nc
    with ExitStack() as ctx:
        keep = ctx.enter_context(tc.tile_pool(name="keep", bufs=1))
        psum = ctx.enter_context(tc.psum_pool(name="psum", bufs=8))

        def load_list(src, name):
            tile = keep.tile([P, S // 16], U16, name=name)
            nc.sync.dma_start(tile[:], src)
            return tile

        def load_columns(w, first, width, name):
            raw = keep.tile([P, PACK, width], F32, name=name)
            nc.sync.dma_start(out=raw[:], in_=w[:, first : first + width].rearrange("(p j) c -> p j c", j=PACK))
            return raw

        def deal(dealt, first, raw, copy):
            ms = slice(first // PACK, (first + raw.shape[2]) // PACK)
            copy(out=dealt[:].rearrange("p (t m j) -> p m t j", t=PACK, j=PACK)[:, ms], in_=raw.rearrange("p j (m t) -> p m t j", t=PACK))

        def quantize(values, name):
            width = values.shape[1] // PACK
            codes = keep.tile([P, width], U32, name=name + "_codes", align_bytes=64)
            scales = keep.tile([P, width], U8, name=name + "_scales", align_bytes=64)
            nc.vector.quantize_mx(out=codes[:].bitcast(FP8X4), scales=scales[:], in_=values)
            return codes, scales

        def product(weight, t, moving, name):
            width = moving[0].shape[1]
            bank = psum.tile([P, width], F32, name=name, tag="bank")
            cols = slice(t * P, (t + 1) * P)
            nc.tensor.matmul_mx(out=bank[:], lhsT=weight[0][:, cols].bitcast(FP8X4), lhsT_scale=weight[1][:, cols],
                                rhs=moving[0][:].bitcast(FP8X4), rhs_scale=moving[1][:], start=True, stop=True)
            return bank

        def pick(window, offsets, dtype, name, tag=None):
            picked = keep.tile([P, S], dtype, name=name, tag=tag or name, align_bytes=64)
            nc.vector.tensor_copy(picked[:], window[:].indirect(offsets[:]))
            return picked

        x_bytes = keep.tile([P, T], U8, name="x_bytes")
        nc.vector.memset(x_bytes[:].bitcast(I32), 0)
        warm = keep.tile([P, 1], F32, name="warm")
        nc.vector.memset(warm[:], 0.0)
        for q in range(4):
            nc.scalar.dma_start(out=x_bytes[32 * q : 32 * q + 4, :].bitcast(I32), in_=x_scales[0, 4 * q : 4 * q + 4, :].bitcast(I32))
        warmed = keep.tile([P, 1], F32, name="warmed")
        nc.scalar.activation(warmed[:], warm[:], ACT.Sigmoid)
        identity = keep.tile([P, P], F32, name="identity")
        make_identity(nc, identity[:])
        two_sb = load_list(two, "two_sb")
        x_codes = keep.tile([P, T], U32, name="x_codes")
        nc.sync.dma_start(out=x_codes[:].bitcast(I32), in_=x_words[0].rearrange("p c r -> p (c r)").bitcast(I32))
        offs_sb = load_list(offs, "offs_sb")
        w2_raw = [load_columns(w2, c * HALF, HALF, f"w2_raw{c}") for c in range(2)]
        w1_raw = [load_columns(w1, c * HALF, HALF, f"w1_raw{c}") for c in range(2)]
        n2_sb = load_list(n2, "n2_sb")
        gain = keep.tile([P, PACK], F32, name="gain")
        nc.sync.dma_start(out=gain[:], in_=gn.rearrange("(p t) o -> p (t o)", t=PACK))
        n1_sb = load_list(n1, "n1_sb")
        w3_raw = load_columns(w3, 0, N, "w3_raw")
        n4_sb = load_list(n4, "n4_sb")
        n5_sb = load_list(n5, "n5_sb")
        n3_sb = load_list(n3, "n3_sb")

        two_codes = pick(x_codes, two_sb, U32, "two_codes")
        two_bytes = pick(x_bytes, two_sb, U8, "two_bytes")
        idx_codes = pick(x_codes, offs_sb, U32, "idx_codes")
        w2_dealt = keep.tile([P, PACK * H], BF16, name="w2_dealt", align_bytes=64)
        for c in range(2):
            deal(w2_dealt, c * HALF, w2_raw[c][:], nc.scalar.copy)
        w2_q = quantize(w2_dealt[:], "w2")
        idx_bytes = pick(x_bytes, offs_sb, U8, "idx_bytes", tag="w2_dealt")
        d_banks = [product(w2_q, t, (two_codes, two_bytes), f"d_bank{t}") for t in range(PACK)]
        w1_dealt = keep.tile([P, PACK * H], BF16, name="w1_dealt", align_bytes=64)
        deal(w1_dealt, 0, w1_raw[0][:], nc.scalar.copy)
        deal(w1_dealt, HALF, w1_raw[1][:], nc.vector.tensor_copy)
        w1_q = quantize(w1_dealt[:], "w1")
        y_banks = [product(w1_q, t, (idx_codes, idx_bytes), f"y_bank{t}") for t in range(PACK)]

        pulled = keep.tile([P, PACK, S], F32, name="pulled")
        stayed = keep.tile([P, PACK, S], F32, name="stayed")
        w3_dealt = keep.tile([P, PACK * N], BF16, name="w3_dealt", align_bytes=64)
        gaps = []

        def gap_of_d(t):
            d_win = keep.tile([P, 2 * S], F32, name=f"d_win{t}")
            d_own = keep.tile([P, S], F32, name=f"d_own{t}")
            nc.scalar.copy(d_win[:, :S], d_banks[t][:])
            nc.scalar.copy(d_own[:], d_banks[t][:])
            gap = keep.tile([P, S], F32, name=f"gap{t}")
            nc.vector.tensor_tensor(gap[:], d_win[:].indirect(n2_sb[:]), d_own[:], ALU.subtract)
            gaps.append(gap)

        def blend_y(t):
            y_win = keep.tile([P, 2 * S], F32, name=f"y_win{t}")
            nc.scalar.activation(y_win[:, :S], y_banks[t][:], ACT.Copy, scale=gain[:, t : t + 1])
            gate = keep.tile([P, S], F32, name=f"gate{t}")
            nc.scalar.activation(gate[:], gaps[t][:], ACT.Sigmoid)
            nc.vector.tensor_tensor(pulled[:, t, :], y_win[:].indirect(n1_sb[:]), gate[:], ALU.mult)
            nc.vector.scalar_tensor_tensor(stayed[:, t, :], gate[:], 1.0, y_win[:, :S], ALU.subtract, ALU.mult)

        gap_of_d(0)

        gap_of_d(1)
        for t in range(PACK):
            blend_y(t)
            if t + 2 < PACK:
                gap_of_d(t + 2)
            deal(w3_dealt, t * P, w3_raw[:, :, t * P : (t + 1) * P], nc.scalar.copy)
        w3_q = quantize(w3_dealt[:], "w3")

        zs = []
        for c in range(2):
            cols = slice(c * HALF, (c + 1) * HALF)
            z = keep.tile([P, HALF * PACK], BF16, name=f"z{c}", align_bytes=64)
            nc.vector.tensor_tensor(
                z[:].rearrange("p (c i t) -> p c t i", i=4, t=PACK),
                pulled[:, :, cols].rearrange("p t (c i) -> p c t i", i=4),
                stayed[:, :, cols].rearrange("p t (c i) -> p c t i", i=4),
                ALU.subtract,
            )
            zs.append(z)
        z_q = [quantize(zs[c][:], f"z{c}") for c in range(2)]

        out_rows = out.rearrange("(p t) j -> t p j", t=PACK)
        fars, nears = [], []
        for t in range(PACK):
            h_win = keep.tile([P, 2 * S], F32, name=f"h_win{t}")
            for c in range(2):
                bank = product(w3_q, t, z_q[c], f"h_bank{c}{t}")
                nc.scalar.copy(h_win[:, c * HALF : (c + 1) * HALF], bank[:])
            mix = keep.tile([P, S], F32, name=f"mix{t}")
            far = keep.tile([P, S], F32, name=f"far{t}")
            near = keep.tile([P, S], F32, name=f"near{t}")
            if t == 0:
                pa = keep.tile([P, S], F32, name="pa")
                nc.vector.tensor_scalar(pa[:], h_win[:].indirect(n3_sb[:]), -1.0, 0.0, ALU.mult, ALU.add)
            nc.scalar.activation(mix[:], h_win[:].indirect(n4_sb[:]), ACT.Sigmoid)
            nc.vector.tensor_tensor(far[:], h_win[:].indirect(n5_sb[:]), mix[:], ALU.mult)
            if t == 0:
                nc.vector.scalar_tensor_tensor(near[:], mix[:], 1.0, pa[:], ALU.subtract, ALU.mult)
            else:
                rest = keep.tile([P, S], F32, name=f"rest{t}")
                nc.scalar.activation(rest[:], mix[:], ACT.Copy, bias=1.0, scale=-1.0)
                nc.vector.tensor_tensor(near[:], h_win[:].indirect(n3_sb[:]), rest[:], ALU.mult)
            fars.append(far)
            nears.append(near)
            if t == 2:
                res = keep.tile([P, S], F32, name="res2")
                nc.vector.tensor_tensor(res[:], far[:], near[:], ALU.add)
                nc.sync.dma_start(out=out_rows[t], in_=res[:])
            if t == 3:
                res = keep.tile([P, S], F32, name="res3")
                for c in range(2):
                    cols = slice(c * HALF, (c + 1) * HALF)
                    nc.vector.tensor_tensor(res[:, cols], far[:, cols], near[:, cols], ALU.add)
                    nc.sync.dma_start(out=out_rows[t][:, cols], in_=res[:, cols])

        blocks = [slice(b * P, (b + 1) * P) for b in range(S // P)]
        turned = []
        for t in range(2):
            bank = psum.tile([P, S], F32, name=f"sum_bank{t}", tag="bank")
            for block in blocks:
                nc.tensor.matmul(bank[:, block], fars[t][:, block], identity[:], start=True, stop=False, is_transpose=True)
                nc.tensor.matmul(bank[:, block], nears[t][:, block], identity[:], start=False, stop=True, is_transpose=True)
            sums = keep.tile([P, S], F32, name=f"sums{t}")
            nc.scalar.copy(sums[:], bank[:])
            turned.append(sums)
        for t in range(2):
            bank = psum.tile([P, S], F32, name=f"back_bank{t}", tag="bank")
            for block in blocks:
                nc.tensor.transpose(bank[:, block], turned[t][:, block], identity[:])
            res = keep.tile([P, S], F32, name=f"res{t}")
            nc.scalar.copy(res[:], bank[:])
            nc.scalar.dma_start(out=out_rows[t], in_=res[:])
